import numpy as np
CORES = [26,90,154,218,282,346,410,474]
N = 8
ROOT = 7
WIDTHS = [4,0,0,0,4,0,2,0]
OFF = [0,4,4,4,4,8,8,10]
C = 10
def setup_inputs(rng):
    return {"x": rng.standard_normal((N, 128, C), dtype=np.float32)}
def reference(x):
    YW = max(WIDTHS)
    y = np.full((N, 128, YW), np.nan, x.dtype)
    for r in range(N):
        y[r][:, :WIDTHS[r]] = x[ROOT][:, OFF[r]:OFF[r] + WIDTHS[r]]
    return {"y": y}

WIDTHS = [4, 0, 0, 0, 4, 0, 2, 0]
ROOT = 7
OFF_CHIP_ENGINES = 8

PIECES = [r for r in range(len(WIDTHS)) if WIDTHS[r] > 0 and r != ROOT]

SCRATCH = {"piece%d" % r: ("dram", [128, WIDTHS[r]], "float32") for r in PIECES}
SEMAPHORES = ["packed%d" % r for r in PIECES] + ["left", "arrived", "stored"]


def _plan(T, topo):
    root = T.cores[ROOT]
    order = sorted(PIECES, key=lambda r: (topo.rack(topo.host(T.cores[r])) == topo.rack(topo.host(root)), -WIDTHS[r], r))
    share = 1
    while share * 2 * len(order) <= OFF_CHIP_ENGINES:
        share *= 2
    free = max(0, OFF_CHIP_ENGINES - share * len(order))
    plan, first = [], 0
    for r in order:
        n = share
        if n <= free:
            free -= n
            n *= 2
        mask = 0
        for e in range(first, first + n):
            mask |= 1 << (e % OFF_CHIP_ENGINES)
        first += n
        plan.append((r, T.cores[r], mask, n))
    return plan


def rank_program(g, core, T, topo):
    rank = T.rank_of(core)
    if rank is None:
        return
    if list(T.tables["WIDTHS"]) != WIDTHS or T.root != ROOT:
        raise ValueError("the buffers declared in SCRATCH are laid out for other tables")
    off = T.tables["OFF"]
    plan = _plan(T, topo)

    if rank == ROOT:
        for i, (r, _dst, _mask, _n) in enumerate(plan):
            q = (g.sync, g.scalar)[i % 2]
            q.dma_start(T["piece%d" % r][:, :], T.x[:, off[r]:off[r] + WIDTHS[r]]).then_inc(T.sem["packed%d" % r], 16)
        for r, dst, mask, _n in plan:
            rid, pid = topo.addr(dst, core)
            g.wait_ge(T.sem["packed%d" % r], 16)
            g.remote_dma(T["piece%d" % r][:, :], T["piece%d" % r][:, :], remote_sem=T.sem.arrived, local_sem=T.sem.left,
                         pid=pid, routing_id=rid, dma_engine_mask=mask)
        g.wait_ge(T.sem.left, sum(n for _r, _dst, _mask, n in plan))
        return

    for r, _dst, _mask, n in plan:
        if r == rank:
            g.sync.wait_ge(T.sem.arrived, n)
            g.sync.dma_start(T.y[:, 0:WIDTHS[r]], T["piece%d" % r][:, :]).then_inc(T.sem.stored, 16)
            g.sync.wait_ge(T.sem.stored, 16)
